import numpy as np
import ml_dtypes


def mxq(x, axis, fmt="e4m3"):
    dtype, down = {"e4m3": (ml_dtypes.float8_e4m3fn, 7), "e5m2": (ml_dtypes.float8_e5m2, 14)}[fmt]
    v = np.moveaxis(np.asarray(x, np.float32).astype(ml_dtypes.bfloat16).astype(np.float64), axis, -1)
    blocks = v.reshape(v.shape[:-1] + (-1, 32))
    amax = np.abs(blocks).max(-1, keepdims=True)
    byte = np.maximum(np.where(amax > 0, np.frexp(amax)[1] - 1 + 127, 0) - down, 1)
    scale = np.exp2(byte - 127.0)
    codes = (blocks / scale).astype(np.float32).astype(dtype).astype(np.float64)
    return np.moveaxis((codes * scale).reshape(v.shape), -1, axis)


WIDE = False


def mx_kscale(k):
    if not WIDE:
        return np.ones(k)
    levels = np.array([10, -10, 5, -5, 0])
    if k % 512:
        return np.exp2(np.random.permutation(np.resize(levels, k // 32))).repeat(32)
    a = np.empty((k // 512, 16))
    for p in range(k // 512):
        a[p, :8] = np.random.permutation(np.resize(levels, 8))
        for g in range(8):
            far = levels[np.abs(levels - a[p, g]) >= 10]
            a[p, g + 8] = far[np.random.randint(len(far))]
    return np.exp2(a.ravel()).repeat(32)


def f64(x):
    return np.asarray(x).astype(np.float64)


def striped(idx):
    return np.tile(idx.reshape(-1, 16).T, (8, 1)).astype(np.uint16)


def unstriped(offs):
    return offs[:16].T.reshape(-1).astype(np.int64)


E2M1 = np.array([0.0, 0.5, 1.0, 1.5, 2.0, 3.0, 4.0, 6.0, -0.0, -0.5, -1.0, -1.5, -2.0, -3.0, -4.0, -6.0])


def pack_weight(w, fmt):
    k, n = w.shape
    w = f64(np.asarray(w, np.float32).astype(ml_dtypes.bfloat16)).reshape(k // 32, 32, n)
    amax = np.abs(w).max(1)
    if fmt == "e4m3":
        byte = np.frexp(amax)[1] - 1 + 127 - 7
    else:
        mant, ex = np.frexp(amax / 6.0)
        byte = np.where(mant > 0.5, ex, ex - 1) + 127
    byte = np.clip(np.where(amax > 0, byte, 1), 1, 254)
    scaled = (w * np.exp2(127.0 - byte)[:, None, :]).reshape(k, n).astype(np.float32)
    by_word = np.ascontiguousarray(scaled.reshape(k // 512, 128, 4, n).transpose(0, 1, 3, 2))
    if fmt == "e4m3":
        words = by_word.astype(ml_dtypes.float8_e4m3fn).view(np.uint8)
    else:
        c = by_word.astype(ml_dtypes.float4_e2m1fn).view(np.uint8) & 0xF
        words = (c[..., 0::2] | (c[..., 1::2] << 4)).reshape(k // 512, 128, 2 * n)
    return np.ascontiguousarray(words), np.ascontiguousarray(byte.astype(np.uint8).reshape(k // 512, 16, n))


def unpack_weight(words, scales, fmt):
    g, _, n = scales.shape
    words = np.ascontiguousarray(words).reshape(g, 128, n, -1)
    if fmt == "e4m3":
        vals = words.view(ml_dtypes.float8_e4m3fn).astype(np.float64)
    else:
        nib = np.empty((g, 128, n, 4), np.uint8)
        nib[..., 0::2] = words & 0xF
        nib[..., 1::2] = words >> 4
        vals = E2M1[nib]
    vals = vals * np.repeat(np.exp2(scales.astype(np.float64) - 127.0), 8, axis=1)[..., None]
    return vals.transpose(0, 1, 3, 2).reshape(g * 512, n)


def gelu(v):
    return 0.5 * v * (1.0 + np.tanh(np.sqrt(2.0 / np.pi) * (v + 0.044715 * v**3)))


K, H, N, T, S, P = 512, 1024, 512, 2048, 1024, 512

def setup_inputs():
    n = np.random.standard_normal
    s = mx_kscale(K)[:, None]
    u = mx_kscale(H)[:, None]
    tab_words, tab_scales = pack_weight(n((K, T)) * s, "e4m3")
    w1 = 0.6 * n((K, H)) / np.sqrt(K) / s
    w2_words, w2_scales = pack_weight(0.6 * n((K, H)) / np.sqrt(K) / s, "e2m1")
    w3 = 0.9 * n((K, H)) / np.sqrt(K) / s * u.T
    gain = np.random.uniform(2.5, 5.0, H) * np.sign(n(H)) * u[:, 0]
    w4_words, w4_scales = pack_weight(n((H, N)) / np.sqrt(H) / u, "e4m3")
    return {
        "tab_words": tab_words, "tab_scales": tab_scales,
        "offs": striped(np.random.permutation(T)[:S]),
        "pos1": striped(np.random.permutation(S)[:P]),
        "pos2": striped(np.random.permutation(S)[:P]),
        "w1": w1.astype(np.float32),
        "w2_words": w2_words, "w2_scales": w2_scales,
        "w3": w3.astype(np.float32),
        "gain": gain.astype(np.float32),
        "w4_words": w4_words, "w4_scales": w4_scales,
    }

def reference(tab_words, tab_scales, offs, pos1, pos2, w1, w2_words, w2_scales, w3, gain, w4_words, w4_scales):
    v = unpack_weight(tab_words, tab_scales, "e4m3")[:, unstriped(offs)]
    w1q = mxq(f64(w1), 0, "e4m3")
    w2 = unpack_weight(w2_words, w2_scales, "e2m1")
    w3q = mxq(f64(w3), 0, "e4m3")
    w4 = unpack_weight(w4_words, w4_scales, "e4m3")
    h = np.abs((w1q.T @ v) - (w2.T @ v))
    g = w3q.T @ v
    top = h.max(axis=1)
    a = np.exp(h[:, unstriped(pos1)] - top[:, None])
    x = f64(gain)[:, None] * a + g[:, unstriped(pos2)]
    xq = mxq(x, 0, "e4m3")
    y = w4.T @ xq
    return np.square(y)

@@ -1,0 +1,243 @@
+from contextlib import ExitStack
+
+import concourse.mybir as mybir
+
+K, H, N, T, S, M = 512, 1024, 512, 2048, 1024, 512
+FLOPS = 3 * 2 * K * H * S + 2 * H * N * M
+
+F32 = mybir.dt.float32
+BF16 = mybir.dt.bfloat16
+I32 = mybir.dt.int32
+U32 = mybir.dt.uint32
+U16 = mybir.dt.uint16
+U8 = mybir.dt.uint8
+FP8X4 = mybir.dt.float8_e4m3fn_x4
+FP4X4 = mybir.dt.float4_e2m1fn_x4
+ACT = mybir.ActivationFunctionType
+ALU = mybir.AluOpType
+AXIS = mybir.AxisListType
+
+P = 128
+PACK = 4
+PASS = P * PACK
+BANK = 512
+PASSES = H // PASS
+TILES = H // P
+HALF = M // 2
+
+
+def tile_list_whitest_patch_score_kernel(
+    tc, tab_words, tab_scales, offs, pos1, pos2, w1, w2_words, w2_scales, w3, gain, w4_words, w4_scales, out
+):
+    nc = tc.nc
+    with ExitStack() as ctx:
+        lists = ctx.enter_context(tc.tile_pool(name="lists", bufs=1))
+        keep = ctx.enter_context(tc.tile_pool(name="keep", bufs=1))
+        psum = ctx.enter_context(tc.psum_pool(name="psum", bufs=1))
+
+        def sb(name, shape, dtype):
+            return keep.tile(shape, dtype, name=name, align_bytes=64)
+
+        offs_sb = lists.tile([P, S // 16], U16, name="offs_sb")
+        pos1_sb = lists.tile([P, M // 16], U16, name="pos1_sb")
+        pos2_sb = lists.tile([P, M // 16], U16, name="pos2_sb")
+
+        tab_w = sb("tab_w", [P, T], I32)
+        tab_s = sb("tab_s", [P, T], U8)
+        w2_w = sb("w2_w", [P, 2 * H], U8)
+        w2_s = sb("w2_s", [P, H], U8)
+        w4_w = sb("w4_w", [P, PASSES, N], I32)
+        w4_s = sb("w4_s", [P, PASSES, N], U8)
+        gain_sb = sb("gain_sb", [P, PASSES, PACK], F32)
+
+        nc.gpsimd.memset(tab_s[:].bitcast(I32), 0)
+        nc.vector.memset(w2_s[:].bitcast(I32), 0)
+        nc.vector.memset(w4_s[:].rearrange("p a n -> p (a n)").bitcast(I32), 0)
+
+        def load_raw(name, w, c0, width):
+            raw = sb(name, [P, PACK, width], F32)
+            nc.sync.dma_start(out=raw[:], in_=w[:, c0 : c0 + width].rearrange("(p j) c -> p j c", j=PACK))
+            return raw
+
+        nc.sync.dma_start(offs_sb[:], offs)
+        nc.sync.dma_start(out=w2_w[:].bitcast(I32), in_=w2_words[0].bitcast(I32))
+        for q in range(4):
+            nc.sync.dma_start(
+                out=tab_s[32 * q : 32 * q + 4, :].bitcast(I32), in_=tab_scales[0, 4 * q : 4 * q + 4, :].bitcast(I32)
+            )
+        nc.sync.dma_start(out=tab_w[:], in_=tab_words[0].rearrange("p t i -> p (t i)").bitcast(I32))
+        for q in range(4):
+            nc.sync.dma_start(
+                out=w2_s[32 * q : 32 * q + 4, :].bitcast(I32), in_=w2_scales[0, 4 * q : 4 * q + 4, :].bitcast(I32)
+            )
+        w1_first = [load_raw(f"w1_first{c}", w1, 256 * c, 256) for c in range(2)]
+        w3_raw0 = load_raw("w3_raw0", w3, 0, PASS)
+        nc.sync.dma_start(pos1_sb[:], pos1)
+        nc.sync.dma_start(pos2_sb[:], pos2)
+        nc.sync.dma_start(out=gain_sb[:], in_=gain.rearrange("(b p t) -> p b t", p=P, t=PACK))
+        w1_raw1 = load_raw("w1_raw1", w1, PASS, PASS)
+        w3_raw1 = load_raw("w3_raw1", w3, PASS, PASS)
+        nc.sync.dma_start(out=w4_w[:], in_=w4_words.rearrange("a p n i -> p a (n i)").bitcast(I32))
+        for q in range(4):
+            nc.sync.dma_start(
+                out=w4_s[32 * q : 32 * q + 4, :, :].bitcast(I32),
+                in_=w4_scales[:, 4 * q : 4 * q + 4, :].rearrange("a r n -> r a n").bitcast(I32),
+            )
+
+        v_w = [sb(f"v_w{u}", [P, BANK], U32) for u in range(2)]
+        v_s = [sb(f"v_s{u}", [P, BANK], U8) for u in range(2)]
+        for u in range(2):
+            nc.vector.tensor_copy(v_s[u][:], tab_s[:].indirect(offs_sb[:, 32 * u : 32 * u + 32]))
+        for u in range(2):
+            nc.vector.tensor_copy(v_w[u][:], tab_w[:].bitcast(U32).indirect(offs_sb[:, 32 * u : 32 * u + 32]))
+
+        w2_wd = sb("w2_wd", [P, 2 * H], U8)
+        w2_sd = sb("w2_sd", [P, H], U8)
+        nc.vector.tensor_copy(
+            out=w2_sd[:].rearrange("p (b t q) -> p b t q", b=PASSES, t=PACK),
+            in_=w2_s[:].rearrange("p (b q t) -> p b t q", b=PASSES, t=PACK),
+        )
+        nc.vector.tensor_copy(
+            out=w2_wd[:].bitcast(U16).rearrange("p (b t q) -> p b t q", b=PASSES, t=PACK),
+            in_=w2_w[:].bitcast(U16).rearrange("p (b q t) -> p b t q", b=PASSES, t=PACK),
+        )
+
+        def grouped_view(grouped, q0, q1):
+            return grouped[:].rearrange("p (t q j) -> p q j t", t=PACK, j=PACK)[:, q0:q1, :, :]
+
+        def raw_view(raw):
+            return raw[:].rearrange("p j (q t) -> p q j t", t=PACK)
+
+        def round_weight(engine, dst, src, sign):
+            if engine == "scalar":
+                nc.scalar.activation(out=dst, in_=src, func=ACT.Copy, scale=sign)
+            elif sign == 1.0:
+                nc.vector.tensor_copy(out=dst, in_=src)
+            else:
+                nc.vector.tensor_scalar(out=dst, in0=src, scalar1=sign, scalar2=None, op0=ALU.mult)
+
+        def quantize(grouped, codes, scales, c0, c1):
+            nc.vector.quantize_mx(
+                out=codes[:, c0:c1].bitcast(FP8X4), scales=scales[:, c0:c1], in_=grouped[:, PACK * c0 : PACK * c1]
+            )
+
+        w1_g = [sb(f"w1_g{b}", [P, PASS * PACK], BF16) for b in range(PASSES)]
+        w3_g = [sb(f"w3_g{b}", [P, PASS * PACK], BF16) for b in range(PASSES)]
+        w1_c = [sb(f"w1_c{b}", [P, PASS], U32) for b in range(PASSES)]
+        w3_c = [sb(f"w3_c{b}", [P, PASS], U32) for b in range(PASSES)]
+        w1_s = [sb(f"w1_s{b}", [P, PASS], U8) for b in range(PASSES)]
+        w3_s = [sb(f"w3_s{b}", [P, PASS], U8) for b in range(PASSES)]
+
+        round_weight("scalar", grouped_view(w1_g[0], 0, 64), raw_view(w1_first[0]), -1.0)
+        round_weight("vector", grouped_view(w1_g[0], 64, 128), raw_view(w1_first[1]), -1.0)
+        quantize(w1_g[0], w1_c[0], w1_s[0], 0, P)
+        quantize(w1_g[0], w1_c[0], w1_s[0], P, PASS)
+
+        h = [sb(f"h{i}", [P, S], F32) for i in range(TILES)]
+        g = [sb(f"g{i}", [P, S], F32) for i in range(TILES)]
+        a = [sb(f"a{i}", [P, M], F32) for i in range(TILES)]
+        gg = [sb(f"gg{i}", [P, M], F32) for i in range(TILES)]
+        neg_top = [sb(f"neg_top{i}", [P, 1], F32) for i in range(TILES)]
+        x = [sb(f"x{b}", [P, PACK, M], F32) for b in range(PASSES)]
+        x_g = [sb(f"x_g{b}", [P, M * PACK], BF16) for b in range(PASSES)]
+        x_c = [sb(f"x_c{b}", [P, M], U32) for b in range(PASSES)]
+        x_s = [sb(f"x_s{b}", [P, M], U8) for b in range(PASSES)]
+
+        def bank(index, name):
+            return psum.tile([P, BANK], F32, name=name, tag=f"bank{index}")
+
+        def make_h(i):
+            b, t = divmod(i, PACK)
+            cols = slice(P * t, P * (t + 1))
+            for u in range(2):
+                acc = bank(2 * (i % 2) + u, f"d{i}_{u}")
+                nc.tensor.matmul_mx(
+                    out=acc[:], lhsT=w1_c[b][:, cols].bitcast(FP8X4), lhsT_scale=w1_s[b][:, cols],
+                    rhs=v_w[u][:].bitcast(FP8X4), rhs_scale=v_s[u][:], start=True, stop=False,
+                )
+                nc.tensor.matmul_mx(
+                    out=acc[:], lhsT=w2_wd[:, 2 * P * i : 2 * P * (i + 1)].bitcast(FP4X4),
+                    lhsT_scale=w2_sd[:, P * i : P * (i + 1)],
+                    rhs=v_w[u][:].bitcast(FP8X4), rhs_scale=v_s[u][:], start=False, stop=True,
+                )
+                nc.scalar.activation(out=h[i][:, BANK * u : BANK * (u + 1)], in_=acc[:], func=ACT.Abs)
+            nc.vector.tensor_reduce(out=neg_top[i][:], in_=h[i][:], axis=AXIS.X, op=ALU.max, negate=True)
+
+        def make_g(i):
+            b, t = divmod(i, PACK)
+            cols = slice(P * t, P * (t + 1))
+            for u in range(2):
+                acc = bank(4 + 2 * (i % 2) + u, f"e{i}_{u}")
+                nc.tensor.matmul_mx(
+                    out=acc[:], lhsT=w3_c[b][:, cols].bitcast(FP8X4), lhsT_scale=w3_s[b][:, cols],
+                    rhs=v_w[u][:].bitcast(FP8X4), rhs_scale=v_s[u][:], start=True, stop=True,
+                )
+                nc.scalar.copy(out=g[i][:, BANK * u : BANK * (u + 1)], in_=acc[:])
+            nc.vector.tensor_copy(gg[i][:], g[i][:].indirect(pos2_sb[:]))
+
+        def look(i):
+            nc.scalar.activation(out=a[i][:], in_=h[i][:].indirect(pos1_sb[:]), func=ACT.Exp, bias=neg_top[i][:])
+
+        def make_x(i):
+            b, t = divmod(i, PACK)
+            nc.vector.scalar_tensor_tensor(
+                out=x[b][:, t, :], in0=a[i][:], scalar=gain_sb[:, b, t : t + 1], in1=gg[i][:],
+                op0=ALU.mult, op1=ALU.add,
+            )
+
+        def round_x(b, m0, m1):
+            nc.vector.tensor_copy(
+                out=x_g[b][:, PACK * m0 : PACK * m1].rearrange("p (c i t) -> p c t i", i=4, t=PACK),
+                in_=x[b][:, :, m0:m1].rearrange("p t (c i) -> p c t i", i=4),
+            )
+
+        make_h(0)
+        round_weight("vector", grouped_view(w3_g[0], 0, P), raw_view(w3_raw0), 1.0)
+        make_h(1)
+        quantize(w3_g[0], w3_c[0], w3_s[0], 0, PASS)
+        for i in range(TILES):
+            make_g(i)
+            look(i)
+            if i + 2 < TILES:
+                make_h(i + 2)
+            make_x(i)
+            if i == 0:
+                round_weight("vector", grouped_view(w1_g[1], 0, P), raw_view(w1_raw1), -1.0)
+            if i == 1:
+                quantize(w1_g[1], w1_c[1], w1_s[1], 0, PASS)
+                round_weight("scalar", grouped_view(w3_g[1], 0, P), raw_view(w3_raw1), 1.0)
+            if i == 2:
+                quantize(w3_g[1], w3_c[1], w3_s[1], 0, PASS)
+            if i == 4:
+                round_x(0, 0, M)
+            if i == 5:
+                quantize(x_g[0], x_c[0], x_s[0], 0, M)
+
+        y = [[bank(2 + 4 * u + k, f"y{u}_{k}") for k in range(2)] for u in range(2)]
+
+        def last_pass(b, u):
+            ms = slice(HALF * u, HALF * (u + 1))
+            for k in range(2):
+                for e in range(2):
+                    ns = slice(P * (2 * k + e), P * (2 * k + e + 1))
+                    nc.tensor.matmul_mx(
+                        out=y[u][k][:, HALF * e : HALF * (e + 1)],
+                        lhsT=w4_w[:, b, ns].bitcast(FP8X4), lhsT_scale=w4_s[:, b, ns],
+                        rhs=x_c[b][:, ms].bitcast(FP8X4), rhs_scale=x_s[b][:, ms],
+                        start=(b == 0 and e == 0), stop=(b == PASSES - 1 and e == 1),
+                    )
+
+        for u in range(2):
+            last_pass(0, u)
+        for u in range(2):
+            round_x(1, HALF * u, HALF * (u + 1))
+        for u in range(2):
+            quantize(x_g[1], x_c[1], x_s[1], HALF * u, HALF * (u + 1))
+            last_pass(1, u)
+            for k in range(2):
+                score = sb(f"score{u}_{k}", [P, 2, HALF], F32)
+                nc.scalar.activation(out=score[:].rearrange("p e m -> p (e m)"), in_=y[u][k][:], func=ACT.Square)
+                nc.sync.dma_start(
+                    out=out[2 * P * k : 2 * P * (k + 1), HALF * u : HALF * (u + 1)].rearrange("(e p) m -> p e m", p=P),
+                    in_=score[:],
+                )

@@ -35,8 +35,8 @@ def tile_list_whitest_patch_score_kernel(
         keep = ctx.enter_context(tc.tile_pool(name="keep", bufs=1))
         psum = ctx.enter_context(tc.psum_pool(name="psum", bufs=1))
 
-        def sb(name, shape, dtype):
-            return keep.tile(shape, dtype, name=name, align_bytes=64)
+        def sb(name, shape, dtype, tag=None):
+            return keep.tile(shape, dtype, name=name, tag=tag or name, align_bytes=64)
 
         offs_sb = lists.tile([P, S // 16], U16, name="offs_sb")
         pos1_sb = lists.tile([P, M // 16], U16, name="pos1_sb")
@@ -50,9 +50,9 @@ def tile_list_whitest_patch_score_kernel(
         w4_s = sb("w4_s", [P, PASSES, N], U8)
         gain_sb = sb("gain_sb", [P, PASSES, PACK], F32)
 
-        nc.gpsimd.memset(tab_s[:].bitcast(I32), 0)
-        nc.vector.memset(w2_s[:].bitcast(I32), 0)
-        nc.vector.memset(w4_s[:].rearrange("p a n -> p (a n)").bitcast(I32), 0)
+        nc.vector.memset(tab_s[:].bitcast(I32), 0)
+        nc.gpsimd.memset(w2_s[:].bitcast(I32), 0)
+        nc.gpsimd.memset(w4_s[:].rearrange("p a n -> p (a n)").bitcast(I32), 0)
 
         def load_raw(name, w, c0, width):
             raw = sb(name, [P, PACK, width], F32)
@@ -60,23 +60,24 @@ def tile_list_whitest_patch_score_kernel(
             return raw
 
         nc.sync.dma_start(offs_sb[:], offs)
-        nc.sync.dma_start(out=w2_w[:].bitcast(I32), in_=w2_words[0].bitcast(I32))
+        w3_first = [load_raw("w3_first0", w3, 0, 256)]
         for q in range(4):
             nc.sync.dma_start(
                 out=tab_s[32 * q : 32 * q + 4, :].bitcast(I32), in_=tab_scales[0, 4 * q : 4 * q + 4, :].bitcast(I32)
             )
         nc.sync.dma_start(out=tab_w[:], in_=tab_words[0].rearrange("p t i -> p (t i)").bitcast(I32))
+        w3_first.append(load_raw("w3_first1", w3, 256, 256))
+        nc.sync.dma_start(pos2_sb[:], pos2)
         for q in range(4):
             nc.sync.dma_start(
                 out=w2_s[32 * q : 32 * q + 4, :].bitcast(I32), in_=w2_scales[0, 4 * q : 4 * q + 4, :].bitcast(I32)
             )
-        w1_first = [load_raw(f"w1_first{c}", w1, 256 * c, 256) for c in range(2)]
-        w3_raw0 = load_raw("w3_raw0", w3, 0, PASS)
+        nc.sync.dma_start(out=w2_w[:].bitcast(I32), in_=w2_words[0].bitcast(I32))
+        w1_raw0 = load_raw("w1_raw0", w1, 0, PASS)
         nc.sync.dma_start(pos1_sb[:], pos1)
-        nc.sync.dma_start(pos2_sb[:], pos2)
         nc.sync.dma_start(out=gain_sb[:], in_=gain.rearrange("(b p t) -> p b t", p=P, t=PACK))
-        w1_raw1 = load_raw("w1_raw1", w1, PASS, PASS)
         w3_raw1 = load_raw("w3_raw1", w3, PASS, PASS)
+        w1_raw1 = load_raw("w1_raw1", w1, PASS, PASS)
         nc.sync.dma_start(out=w4_w[:], in_=w4_words.rearrange("a p n i -> p a (n i)").bitcast(I32))
         for q in range(4):
             nc.sync.dma_start(
@@ -93,14 +94,16 @@ def tile_list_whitest_patch_score_kernel(
 
         w2_wd = sb("w2_wd", [P, 2 * H], U8)
         w2_sd = sb("w2_sd", [P, H], U8)
-        nc.vector.tensor_copy(
-            out=w2_sd[:].rearrange("p (b t q) -> p b t q", b=PASSES, t=PACK),
-            in_=w2_s[:].rearrange("p (b q t) -> p b t q", b=PASSES, t=PACK),
-        )
-        nc.vector.tensor_copy(
-            out=w2_wd[:].bitcast(U16).rearrange("p (b t q) -> p b t q", b=PASSES, t=PACK),
-            in_=w2_w[:].bitcast(U16).rearrange("p (b q t) -> p b t q", b=PASSES, t=PACK),
-        )
+
+        def deal_w2():
+            nc.vector.tensor_copy(
+                out=w2_sd[:].rearrange("p (b t q) -> p b t q", b=PASSES, t=PACK),
+                in_=w2_s[:].rearrange("p (b q t) -> p b t q", b=PASSES, t=PACK),
+            )
+            nc.scalar.copy(
+                out=w2_wd[:].bitcast(U16).rearrange("p (b t q) -> p b t q", b=PASSES, t=PACK),
+                in_=w2_w[:].bitcast(U16).rearrange("p (b q t) -> p b t q", b=PASSES, t=PACK),
+            )
 
         def grouped_view(grouped, q0, q1):
             return grouped[:].rearrange("p (t q j) -> p q j t", t=PACK, j=PACK)[:, q0:q1, :, :]
@@ -111,6 +114,8 @@ def tile_list_whitest_patch_score_kernel(
         def round_weight(engine, dst, src, sign):
             if engine == "scalar":
                 nc.scalar.activation(out=dst, in_=src, func=ACT.Copy, scale=sign)
+            elif engine == "gpsimd":
+                nc.gpsimd.tensor_scalar(out=dst, in0=src, scalar1=sign, scalar2=0.0, op0=ALU.mult, op1=ALU.add)
             elif sign == 1.0:
                 nc.vector.tensor_copy(out=dst, in_=src)
             else:
@@ -128,29 +133,34 @@ def tile_list_whitest_patch_score_kernel(
         w1_s = [sb(f"w1_s{b}", [P, PASS], U8) for b in range(PASSES)]
         w3_s = [sb(f"w3_s{b}", [P, PASS], U8) for b in range(PASSES)]
 
-        round_weight("scalar", grouped_view(w1_g[0], 0, 64), raw_view(w1_first[0]), -1.0)
-        round_weight("vector", grouped_view(w1_g[0], 64, 128), raw_view(w1_first[1]), -1.0)
-        quantize(w1_g[0], w1_c[0], w1_s[0], 0, P)
-        quantize(w1_g[0], w1_c[0], w1_s[0], P, PASS)
+        round_weight("scalar", grouped_view(w3_g[0], 0, 64), raw_view(w3_first[0]), 1.0)
+        round_weight("scalar", grouped_view(w3_g[0], 64, 128), raw_view(w3_first[1]), 1.0)
+        quantize(w3_g[0], w3_c[0], w3_s[0], 0, P)
+        quantize(w3_g[0], w3_c[0], w3_s[0], P, PASS)
 
         h = [sb(f"h{i}", [P, S], F32) for i in range(TILES)]
         g = [sb(f"g{i}", [P, S], F32) for i in range(TILES)]
         a = [sb(f"a{i}", [P, M], F32) for i in range(TILES)]
-        gg = [sb(f"gg{i}", [P, M], F32) for i in range(TILES)]
         neg_top = [sb(f"neg_top{i}", [P, 1], F32) for i in range(TILES)]
         x = [sb(f"x{b}", [P, PACK, M], F32) for b in range(PASSES)]
         x_g = [sb(f"x_g{b}", [P, M * PACK], BF16) for b in range(PASSES)]
-        x_c = [sb(f"x_c{b}", [P, M], U32) for b in range(PASSES)]
         x_s = [sb(f"x_s{b}", [P, M], U8) for b in range(PASSES)]
 
         def bank(index, name):
             return psum.tile([P, BANK], F32, name=name, tag=f"bank{index}")
 
+        uses = [("g", 0), ("g", 1)]
+        for i in range(TILES):
+            uses.append(("h", i))
+            if i + 2 < TILES:
+                uses.append(("g", i + 2))
+        ring = {use: n % 3 for n, use in enumerate(uses)}
+
         def make_h(i):
             b, t = divmod(i, PACK)
             cols = slice(P * t, P * (t + 1))
             for u in range(2):
-                acc = bank(2 * (i % 2) + u, f"d{i}_{u}")
+                acc = bank(2 * ring[("h", i)] + u, f"d{i}_{u}")
                 nc.tensor.matmul_mx(
                     out=acc[:], lhsT=w1_c[b][:, cols].bitcast(FP8X4), lhsT_scale=w1_s[b][:, cols],
                     rhs=v_w[u][:].bitcast(FP8X4), rhs_scale=v_s[u][:], start=True, stop=False,
@@ -167,77 +177,94 @@ def tile_list_whitest_patch_score_kernel(
             b, t = divmod(i, PACK)
             cols = slice(P * t, P * (t + 1))
             for u in range(2):
-                acc = bank(4 + 2 * (i % 2) + u, f"e{i}_{u}")
+                acc = bank(2 * ring[("g", i)] + u, f"e{i}_{u}")
                 nc.tensor.matmul_mx(
                     out=acc[:], lhsT=w3_c[b][:, cols].bitcast(FP8X4), lhsT_scale=w3_s[b][:, cols],
                     rhs=v_w[u][:].bitcast(FP8X4), rhs_scale=v_s[u][:], start=True, stop=True,
                 )
                 nc.scalar.copy(out=g[i][:, BANK * u : BANK * (u + 1)], in_=acc[:])
-            nc.vector.tensor_copy(gg[i][:], g[i][:].indirect(pos2_sb[:]))
+            nc.vector.tensor_copy(gg[i], g[i][:].indirect(pos2_sb[:]))
 
-        def look(i):
-            nc.scalar.activation(out=a[i][:], in_=h[i][:].indirect(pos1_sb[:]), func=ACT.Exp, bias=neg_top[i][:])
+        def look(i, m0, m1):
+            nc.scalar.activation(
+                out=a[i][:, m0:m1], in_=h[i][:].indirect(pos1_sb[:, m0 // 16 : m1 // 16]), func=ACT.Exp,
+                bias=neg_top[i][:],
+            )
 
-        def make_x(i):
+        def make_x(i, m0, m1):
             b, t = divmod(i, PACK)
             nc.vector.scalar_tensor_tensor(
-                out=x[b][:, t, :], in0=a[i][:], scalar=gain_sb[:, b, t : t + 1], in1=gg[i][:],
+                out=x[b][:, t, m0:m1], in0=a[i][:, m0:m1], scalar=gain_sb[:, b, t : t + 1], in1=gg[i][:, m0:m1],
                 op0=ALU.mult, op1=ALU.add,
             )
 
-        def round_x(b, m0, m1):
-            nc.vector.tensor_copy(
-                out=x_g[b][:, PACK * m0 : PACK * m1].rearrange("p (c i t) -> p c t i", i=4, t=PACK),
-                in_=x[b][:, :, m0:m1].rearrange("p t (c i) -> p c t i", i=4),
+        def round_x(engine, b, m0, m1):
+            round_weight(
+                engine,
+                x_g[b][:, PACK * m0 : PACK * m1].rearrange("p (c i t) -> p c t i", i=4, t=PACK),
+                x[b][:, :, m0:m1].rearrange("p t (c i) -> p c t i", i=4),
+                1.0,
             )
 
+        deal_w2()
+        round_weight("vector", grouped_view(w1_g[0], 0, P), raw_view(w1_raw0), -1.0)
+        quantize(w1_g[0], w1_c[0], w1_s[0], 0, P)
+        quantize(w1_g[0], w1_c[0], w1_s[0], P, PASS)
+        gg01 = sb("gg01", [P, 2, M], F32, tag="w1_g0")
+        gg = [gg01[:, 0, :], gg01[:, 1, :], sb("gg2", [P, M], F32, tag="w1_raw0")[:]]
+        gg = gg + [sb(f"gg{i}", [P, M], F32)[:] for i in range(3, TILES)]
+        make_g(0)
+        make_g(1)
         make_h(0)
-        round_weight("vector", grouped_view(w3_g[0], 0, P), raw_view(w3_raw0), 1.0)
-        make_h(1)
-        quantize(w3_g[0], w3_c[0], w3_s[0], 0, PASS)
-        for i in range(TILES):
-            make_g(i)
-            look(i)
-            if i + 2 < TILES:
-                make_h(i + 2)
-            make_x(i)
+        make_g(2)
+        for i in range(TILES - 1):
+            make_h(i + 1)
+            look(i, 0, M)
+            if i + 3 < TILES:
+                make_g(i + 3)
+            make_x(i, 0, M)
             if i == 0:
-                round_weight("vector", grouped_view(w1_g[1], 0, P), raw_view(w1_raw1), -1.0)
-            if i == 1:
-                quantize(w1_g[1], w1_c[1], w1_s[1], 0, PASS)
                 round_weight("scalar", grouped_view(w3_g[1], 0, P), raw_view(w3_raw1), 1.0)
-            if i == 2:
                 quantize(w3_g[1], w3_c[1], w3_s[1], 0, PASS)
-            if i == 4:
-                round_x(0, 0, M)
+            if i == 1:
+                round_weight("vector", grouped_view(w1_g[1], 0, P), raw_view(w1_raw1), -1.0)
+            if i == 2:
+                quantize(w1_g[1], w1_c[1], w1_s[1], 0, PASS)
+            if i == 3:
+                round_x("vector", 0, 0, M)
             if i == 5:
+                x_c = [sb("x_c0", [P, M], U32, tag="gg5"), sb("x_c1", [P, M], U32)]
                 quantize(x_g[0], x_c[0], x_s[0], 0, M)
 
-        y = [[bank(2 + 4 * u + k, f"y{u}_{k}") for k in range(2)] for u in range(2)]
+        y = [bank(index, f"y{n}") for n, index in enumerate((6, 7, 2 * ring[("h", TILES - 2)], 2 * ring[("h", TILES - 2)] + 1))]
 
-        def last_pass(b, u):
-            ms = slice(HALF * u, HALF * (u + 1))
-            for k in range(2):
-                for e in range(2):
-                    ns = slice(P * (2 * k + e), P * (2 * k + e + 1))
-                    nc.tensor.matmul_mx(
-                        out=y[u][k][:, HALF * e : HALF * (e + 1)],
-                        lhsT=w4_w[:, b, ns].bitcast(FP8X4), lhsT_scale=w4_s[:, b, ns],
-                        rhs=x_c[b][:, ms].bitcast(FP8X4), rhs_scale=x_s[b][:, ms],
-                        start=(b == 0 and e == 0), stop=(b == PASSES - 1 and e == 1),
-                    )
-
-        for u in range(2):
-            last_pass(0, u)
-        for u in range(2):
-            round_x(1, HALF * u, HALF * (u + 1))
-        for u in range(2):
-            quantize(x_g[1], x_c[1], x_s[1], HALF * u, HALF * (u + 1))
-            last_pass(1, u)
-            for k in range(2):
-                score = sb(f"score{u}_{k}", [P, 2, HALF], F32)
-                nc.scalar.activation(out=score[:].rearrange("p e m -> p (e m)"), in_=y[u][k][:], func=ACT.Square)
-                nc.sync.dma_start(
-                    out=out[2 * P * k : 2 * P * (k + 1), HALF * u : HALF * (u + 1)].rearrange("(e p) m -> p e m", p=P),
-                    in_=score[:],
+        def last_pass(b, n):
+            ms = slice(P * n, P * (n + 1))
+            for nt in range(N // P):
+                ns = slice(P * nt, P * (nt + 1))
+                nc.tensor.matmul_mx(
+                    out=y[n][:, ns],
+                    lhsT=w4_w[:, b, ns].bitcast(FP8X4), lhsT_scale=w4_s[:, b, ns],
+                    rhs=x_c[b][:, ms].bitcast(FP8X4), rhs_scale=x_s[b][:, ms],
+                    start=(b == 0 and nt == 0), stop=(b == PASSES - 1 and nt == N // P - 1),
                 )
+
+        def finish(n):
+            quantize(x_g[1], x_c[1], x_s[1], P * n, P * (n + 1))
+            last_pass(1, n)
+            score = sb(f"score{n}", [P, N // P, P], F32)
+            nc.scalar.activation(out=score[:].rearrange("p e m -> p (e m)"), in_=y[n][:], func=ACT.Square)
+            queue = nc.scalar if n == 3 else nc.sync
+            queue.dma_start(out=out[:, P * n : P * (n + 1)].rearrange("(e p) m -> p e m", p=P), in_=score[:])
+
+        for n in range(4):
+            last_pass(0, n)
+        last = TILES - 1
+        look(last, 0, HALF)
+        look(last, HALF, M)
+        for u in range(2):
+            make_x(last, HALF * u, HALF * (u + 1))
+            for n in (2 * u, 2 * u + 1):
+                round_x("vector", 1, P * n, P * (n + 1))
+            for n in (2 * u, 2 * u + 1):
+                finish(n)

@@ -76,8 +76,8 @@ def tile_list_whitest_patch_score_kernel(
         w1_raw0 = load_raw("w1_raw0", w1, 0, PASS)
         nc.sync.dma_start(pos1_sb[:], pos1)
         nc.sync.dma_start(out=gain_sb[:], in_=gain.rearrange("(b p t) -> p b t", p=P, t=PACK))
-        w3_raw1 = load_raw("w3_raw1", w3, PASS, PASS)
         w1_raw1 = load_raw("w1_raw1", w1, PASS, PASS)
+        w3_raw1 = load_raw("w3_raw1", w3, PASS, PASS)
         nc.sync.dma_start(out=w4_w[:], in_=w4_words.rearrange("a p n i -> p a (n i)").bitcast(I32))
         for q in range(4):
             nc.sync.dma_start(
@@ -210,6 +210,9 @@ def tile_list_whitest_patch_score_kernel(
         round_weight("vector", grouped_view(w1_g[0], 0, P), raw_view(w1_raw0), -1.0)
         quantize(w1_g[0], w1_c[0], w1_s[0], 0, P)
         quantize(w1_g[0], w1_c[0], w1_s[0], P, PASS)
+        for part in range(4):
+            q0, q1 = 32 * part, 32 * part + 32
+            round_weight("gpsimd", grouped_view(w1_g[1], q0, q1), raw_view(w1_raw1)[:, q0:q1, :, :], -1.0)
         gg01 = sb("gg01", [P, 2, M], F32, tag="w1_g0")
         gg = [gg01[:, 0, :], gg01[:, 1, :], sb("gg2", [P, M], F32, tag="w1_raw0")[:]]
         gg = gg + [sb(f"gg{i}", [P, M], F32)[:] for i in range(3, TILES)]
@@ -217,24 +220,29 @@ def tile_list_whitest_patch_score_kernel(
         make_g(1)
         make_h(0)
         make_g(2)
-        for i in range(TILES - 1):
+        whole = TILES - 3
+        for i in range(whole):
             make_h(i + 1)
             look(i, 0, M)
             if i + 3 < TILES:
                 make_g(i + 3)
             make_x(i, 0, M)
             if i == 0:
-                round_weight("scalar", grouped_view(w3_g[1], 0, P), raw_view(w3_raw1), 1.0)
+                round_weight("scalar", grouped_view(w3_g[1], 0, 64), raw_view(w3_raw1)[:, 0:64, :, :], 1.0)
+                round_weight("vector", grouped_view(w3_g[1], 64, P), raw_view(w3_raw1)[:, 64:P, :, :], 1.0)
                 quantize(w3_g[1], w3_c[1], w3_s[1], 0, PASS)
-            if i == 1:
-                round_weight("vector", grouped_view(w1_g[1], 0, P), raw_view(w1_raw1), -1.0)
             if i == 2:
                 quantize(w1_g[1], w1_c[1], w1_s[1], 0, PASS)
             if i == 3:
-                round_x("vector", 0, 0, M)
-            if i == 5:
-                x_c = [sb("x_c0", [P, M], U32, tag="gg5"), sb("x_c1", [P, M], U32)]
-                quantize(x_g[0], x_c[0], x_s[0], 0, M)
+                for part in range(2):
+                    round_x("gpsimd", 0, P * part, P * part + P)
+                round_x("vector", 0, 2 * P, M)
+        for i in range(whole + 1, TILES):
+            make_h(i)
+        for i in range(whole + 3, TILES):
+            make_g(i)
+        x_c = [sb("x_c0", [P, M], U32, tag="gg4"), sb("x_c1", [P, M], U32)]
+        quantize(x_g[0], x_c[0], x_s[0], 0, M)
 
         y = [bank(index, f"y{n}") for n, index in enumerate((6, 7, 2 * ring[("h", TILES - 2)], 2 * ring[("h", TILES - 2)] + 1))]
 
@@ -259,12 +267,11 @@ def tile_list_whitest_patch_score_kernel(
 
         for n in range(4):
             last_pass(0, n)
-        last = TILES - 1
-        look(last, 0, HALF)
-        look(last, HALF, M)
         for u in range(2):
-            make_x(last, HALF * u, HALF * (u + 1))
+            for i in range(whole, TILES):
+                look(i, HALF * u, HALF * (u + 1))
+                make_x(i, HALF * u, HALF * (u + 1))
             for n in (2 * u, 2 * u + 1):
-                round_x("vector", 1, P * n, P * (n + 1))
+                round_x("scalar" if n in [1,3] else "vector", 1, P * n, P * (n + 1))
             for n in (2 * u, 2 * u + 1):
                 finish(n)

from contextlib import ExitStack

import concourse.mybir as mybir

K, H, N, T, S, M = 512, 1024, 512, 2048, 1024, 512
FLOPS = 3 * 2 * K * H * S + 2 * H * N * M

F32 = mybir.dt.float32
BF16 = mybir.dt.bfloat16
I32 = mybir.dt.int32
U32 = mybir.dt.uint32
U16 = mybir.dt.uint16
U8 = mybir.dt.uint8
FP8X4 = mybir.dt.float8_e4m3fn_x4
FP4X4 = mybir.dt.float4_e2m1fn_x4
ACT = mybir.ActivationFunctionType
ALU = mybir.AluOpType
AXIS = mybir.AxisListType

P = 128
PACK = 4
PASS = P * PACK
BANK = 512
PASSES = H // PASS
TILES = H // P
HALF = M // 2


def tile_list_whitest_patch_score_kernel(
    tc, tab_words, tab_scales, offs, pos1, pos2, w1, w2_words, w2_scales, w3, gain, w4_words, w4_scales, out
):
    nc = tc.nc
    with ExitStack() as ctx:
        lists = ctx.enter_context(tc.tile_pool(name="lists", bufs=1))
        keep = ctx.enter_context(tc.tile_pool(name="keep", bufs=1))
        psum = ctx.enter_context(tc.psum_pool(name="psum", bufs=1))

        def sb(name, shape, dtype, tag=None):
            return keep.tile(shape, dtype, name=name, tag=tag or name, align_bytes=64)

        offs_sb = lists.tile([P, S // 16], U16, name="offs_sb")
        pos1_sb = lists.tile([P, M // 16], U16, name="pos1_sb")
        pos2_sb = lists.tile([P, M // 16], U16, name="pos2_sb")

        tab_w = sb("tab_w", [P, T], I32)
        tab_s = sb("tab_s", [P, T], U8)
        w2_w = sb("w2_w", [P, 2 * H], U8)
        w2_s = sb("w2_s", [P, H], U8)
        w4_w = sb("w4_w", [P, PASSES, N], I32)
        w4_s = sb("w4_s", [P, PASSES, N], U8)
        gain_sb = sb("gain_sb", [P, PASSES, PACK], F32)

        nc.vector.memset(tab_s[:].bitcast(I32), 0)
        nc.gpsimd.memset(w2_s[:].bitcast(I32), 0)
        nc.gpsimd.memset(w4_s[:].rearrange("p a n -> p (a n)").bitcast(I32), 0)

        def load_raw(name, w, c0, width):
            raw = sb(name, [P, PACK, width], F32)
            nc.sync.dma_start(out=raw[:], in_=w[:, c0 : c0 + width].rearrange("(p j) c -> p j c", j=PACK))
            return raw

        nc.sync.dma_start(offs_sb[:], offs)
        w3_first = [load_raw("w3_first0", w3, 0, 256)]
        for q in range(4):
            nc.sync.dma_start(
                out=tab_s[32 * q : 32 * q + 4, :].bitcast(I32), in_=tab_scales[0, 4 * q : 4 * q + 4, :].bitcast(I32)
            )
        nc.sync.dma_start(out=tab_w[:], in_=tab_words[0].rearrange("p t i -> p (t i)").bitcast(I32))
        w3_first.append(load_raw("w3_first1", w3, 256, 256))
        nc.sync.dma_start(pos2_sb[:], pos2)
        for q in range(4):
            nc.sync.dma_start(
                out=w2_s[32 * q : 32 * q + 4, :].bitcast(I32), in_=w2_scales[0, 4 * q : 4 * q + 4, :].bitcast(I32)
            )
        nc.sync.dma_start(out=w2_w[:].bitcast(I32), in_=w2_words[0].bitcast(I32))
        w1_raw0 = load_raw("w1_raw0", w1, 0, PASS)
        nc.sync.dma_start(pos1_sb[:], pos1)
        nc.sync.dma_start(out=gain_sb[:], in_=gain.rearrange("(b p t) -> p b t", p=P, t=PACK))
        w1_raw1 = load_raw("w1_raw1", w1, PASS, PASS)
        w3_raw1 = load_raw("w3_raw1", w3, PASS, PASS)
        nc.sync.dma_start(out=w4_w[:], in_=w4_words.rearrange("a p n i -> p a (n i)").bitcast(I32))
        for q in range(4):
            nc.sync.dma_start(
                out=w4_s[32 * q : 32 * q + 4, :, :].bitcast(I32),
                in_=w4_scales[:, 4 * q : 4 * q + 4, :].rearrange("a r n -> r a n").bitcast(I32),
            )

        v_w = [sb(f"v_w{u}", [P, BANK], U32) for u in range(2)]
        v_s = [sb(f"v_s{u}", [P, BANK], U8) for u in range(2)]
        for u in range(2):
            nc.vector.tensor_copy(v_s[u][:], tab_s[:].indirect(offs_sb[:, 32 * u : 32 * u + 32]))
        for u in range(2):
            nc.vector.tensor_copy(v_w[u][:], tab_w[:].bitcast(U32).indirect(offs_sb[:, 32 * u : 32 * u + 32]))

        w2_wd = sb("w2_wd", [P, 2 * H], U8)
        w2_sd = sb("w2_sd", [P, H], U8)

        def deal_w2():
            nc.vector.tensor_copy(
                out=w2_sd[:].rearrange("p (b t q) -> p b t q", b=PASSES, t=PACK),
                in_=w2_s[:].rearrange("p (b q t) -> p b t q", b=PASSES, t=PACK),
            )
            nc.scalar.copy(
                out=w2_wd[:].bitcast(U16).rearrange("p (b t q) -> p b t q", b=PASSES, t=PACK),
                in_=w2_w[:].bitcast(U16).rearrange("p (b q t) -> p b t q", b=PASSES, t=PACK),
            )

        def grouped_view(grouped, q0, q1):
            return grouped[:].rearrange("p (t q j) -> p q j t", t=PACK, j=PACK)[:, q0:q1, :, :]

        def raw_view(raw):
            return raw[:].rearrange("p j (q t) -> p q j t", t=PACK)

        def round_weight(engine, dst, src, sign):
            if engine == "scalar":
                nc.scalar.activation(out=dst, in_=src, func=ACT.Copy, scale=sign)
            elif engine == "gpsimd":
                nc.gpsimd.tensor_scalar(out=dst, in0=src, scalar1=sign, scalar2=0.0, op0=ALU.mult, op1=ALU.add)
            elif sign == 1.0:
                nc.vector.tensor_copy(out=dst, in_=src)
            else:
                nc.vector.tensor_scalar(out=dst, in0=src, scalar1=sign, scalar2=None, op0=ALU.mult)

        def quantize(grouped, codes, scales, c0, c1):
            nc.vector.quantize_mx(
                out=codes[:, c0:c1].bitcast(FP8X4), scales=scales[:, c0:c1], in_=grouped[:, PACK * c0 : PACK * c1]
            )

        w1_g = [sb(f"w1_g{b}", [P, PASS * PACK], BF16) for b in range(PASSES)]
        w3_g = [sb(f"w3_g{b}", [P, PASS * PACK], BF16) for b in range(PASSES)]
        w1_c = [sb(f"w1_c{b}", [P, PASS], U32) for b in range(PASSES)]
        w3_c = [sb(f"w3_c{b}", [P, PASS], U32) for b in range(PASSES)]
        w1_s = [sb(f"w1_s{b}", [P, PASS], U8) for b in range(PASSES)]
        w3_s = [sb(f"w3_s{b}", [P, PASS], U8) for b in range(PASSES)]

        round_weight("scalar", grouped_view(w3_g[0], 0, 64), raw_view(w3_first[0]), 1.0)
        round_weight("scalar", grouped_view(w3_g[0], 64, 128), raw_view(w3_first[1]), 1.0)
        quantize(w3_g[0], w3_c[0], w3_s[0], 0, P)
        quantize(w3_g[0], w3_c[0], w3_s[0], P, PASS)

        h = [sb(f"h{i}", [P, S], F32) for i in range(TILES)]
        g = [sb(f"g{i}", [P, S], F32) for i in range(TILES)]
        a = [sb(f"a{i}", [P, M], F32) for i in range(TILES)]
        neg_top = [sb(f"neg_top{i}", [P, 1], F32) for i in range(TILES)]
        x = [sb(f"x{b}", [P, PACK, M], F32) for b in range(PASSES)]
        x_g = [sb(f"x_g{b}", [P, M * PACK], BF16) for b in range(PASSES)]
        x_s = [sb(f"x_s{b}", [P, M], U8) for b in range(PASSES)]

        def bank(index, name):
            return psum.tile([P, BANK], F32, name=name, tag=f"bank{index}")

        uses = [("g", 0), ("g", 1)]
        for i in range(TILES):
            uses.append(("h", i))
            if i + 2 < TILES:
                uses.append(("g", i + 2))
        ring = {use: n % 3 for n, use in enumerate(uses)}

        def make_h(i):
            b, t = divmod(i, PACK)
            cols = slice(P * t, P * (t + 1))
            for u in range(2):
                acc = bank(2 * ring[("h", i)] + u, f"d{i}_{u}")
                nc.tensor.matmul_mx(
                    out=acc[:], lhsT=w1_c[b][:, cols].bitcast(FP8X4), lhsT_scale=w1_s[b][:, cols],
                    rhs=v_w[u][:].bitcast(FP8X4), rhs_scale=v_s[u][:], start=True, stop=False,
                )
                nc.tensor.matmul_mx(
                    out=acc[:], lhsT=w2_wd[:, 2 * P * i : 2 * P * (i + 1)].bitcast(FP4X4),
                    lhsT_scale=w2_sd[:, P * i : P * (i + 1)],
                    rhs=v_w[u][:].bitcast(FP8X4), rhs_scale=v_s[u][:], start=False, stop=True,
                )
                nc.scalar.activation(out=h[i][:, BANK * u : BANK * (u + 1)], in_=acc[:], func=ACT.Abs)
            nc.vector.tensor_reduce(out=neg_top[i][:], in_=h[i][:], axis=AXIS.X, op=ALU.max, negate=True)

        def make_g(i):
            b, t = divmod(i, PACK)
            cols = slice(P * t, P * (t + 1))
            for u in range(2):
                acc = bank(2 * ring[("g", i)] + u, f"e{i}_{u}")
                nc.tensor.matmul_mx(
                    out=acc[:], lhsT=w3_c[b][:, cols].bitcast(FP8X4), lhsT_scale=w3_s[b][:, cols],
                    rhs=v_w[u][:].bitcast(FP8X4), rhs_scale=v_s[u][:], start=True, stop=True,
                )
                nc.scalar.copy(out=g[i][:, BANK * u : BANK * (u + 1)], in_=acc[:])
            nc.vector.tensor_copy(gg[i], g[i][:].indirect(pos2_sb[:]))

        def look(i, m0, m1):
            nc.scalar.activation(
                out=a[i][:, m0:m1], in_=h[i][:].indirect(pos1_sb[:, m0 // 16 : m1 // 16]), func=ACT.Exp,
                bias=neg_top[i][:],
            )

        def make_x(i, m0, m1):
            b, t = divmod(i, PACK)
            nc.vector.scalar_tensor_tensor(
                out=x[b][:, t, m0:m1], in0=a[i][:, m0:m1], scalar=gain_sb[:, b, t : t + 1], in1=gg[i][:, m0:m1],
                op0=ALU.mult, op1=ALU.add,
            )

        def round_x(engine, b, m0, m1):
            round_weight(
                engine,
                x_g[b][:, PACK * m0 : PACK * m1].rearrange("p (c i t) -> p c t i", i=4, t=PACK),
                x[b][:, :, m0:m1].rearrange("p t (c i) -> p c t i", i=4),
                1.0,
            )

        deal_w2()
        round_weight("vector", grouped_view(w1_g[0], 0, P), raw_view(w1_raw0), -1.0)
        quantize(w1_g[0], w1_c[0], w1_s[0], 0, P)
        quantize(w1_g[0], w1_c[0], w1_s[0], P, PASS)
        for part in range(4):
            q0, q1 = 32 * part, 32 * part + 32
            round_weight("gpsimd", grouped_view(w1_g[1], q0, q1), raw_view(w1_raw1)[:, q0:q1, :, :], -1.0)
        gg01 = sb("gg01", [P, 2, M], F32, tag="w1_g0")
        gg = [gg01[:, 0, :], gg01[:, 1, :], sb("gg2", [P, M], F32, tag="w1_raw0")[:]]
        gg = gg + [sb(f"gg{i}", [P, M], F32)[:] for i in range(3, TILES)]
        make_g(0)
        make_g(1)
        make_h(0)
        make_g(2)
        whole = TILES - 3
        for i in range(whole):
            make_h(i + 1)
            look(i, 0, M)
            if i + 3 < TILES:
                make_g(i + 3)
            make_x(i, 0, M)
            if i == 0:
                round_weight("scalar", grouped_view(w3_g[1], 0, 64), raw_view(w3_raw1)[:, 0:64, :, :], 1.0)
                round_weight("vector", grouped_view(w3_g[1], 64, P), raw_view(w3_raw1)[:, 64:P, :, :], 1.0)
                quantize(w3_g[1], w3_c[1], w3_s[1], 0, PASS)
            if i == 2:
                quantize(w1_g[1], w1_c[1], w1_s[1], 0, PASS)
            if i == 3:
                for part in range(2):
                    round_x("gpsimd", 0, P * part, P * part + P)
                round_x("vector", 0, 2 * P, M)
        for i in range(whole + 1, TILES):
            make_h(i)
        for i in range(whole + 3, TILES):
            make_g(i)
        x_c = [sb("x_c0", [P, M], U32, tag="gg4"), sb("x_c1", [P, M], U32)]
        quantize(x_g[0], x_c[0], x_s[0], 0, M)

        y = [bank(index, f"y{n}") for n, index in enumerate((6, 7, 2 * ring[("h", TILES - 2)], 2 * ring[("h", TILES - 2)] + 1))]

        def last_pass(b, n):
            ms = slice(P * n, P * (n + 1))
            for nt in range(N // P):
                ns = slice(P * nt, P * (nt + 1))
                nc.tensor.matmul_mx(
                    out=y[n][:, ns],
                    lhsT=w4_w[:, b, ns].bitcast(FP8X4), lhsT_scale=w4_s[:, b, ns],
                    rhs=x_c[b][:, ms].bitcast(FP8X4), rhs_scale=x_s[b][:, ms],
                    start=(b == 0 and nt == 0), stop=(b == PASSES - 1 and nt == N // P - 1),
                )

        def finish(n):
            quantize(x_g[1], x_c[1], x_s[1], P * n, P * (n + 1))
            last_pass(1, n)
            score = sb(f"score{n}", [P, N // P, P], F32)
            nc.scalar.activation(out=score[:].rearrange("p e m -> p (e m)"), in_=y[n][:], func=ACT.Square)
            queue = nc.scalar if n == 3 else nc.sync
            queue.dma_start(out=out[:, P * n : P * (n + 1)].rearrange("(e p) m -> p e m", p=P), in_=score[:])

        for n in range(4):
            last_pass(0, n)
        for u in range(2):
            for i in range(whole, TILES):
                look(i, HALF * u, HALF * (u + 1))
                make_x(i, HALF * u, HALF * (u + 1))
            for n in (2 * u, 2 * u + 1):
                round_x("scalar" if n in [1,3] else "vector", 1, P * n, P * (n + 1))
            for n in (2 * u, 2 * u + 1):
                finish(n)
